import numpy as np
import ml_dtypes


def mxq(x, axis, fmt="e4m3"):
    dtype, down = {"e4m3": (ml_dtypes.float8_e4m3fn, 7), "e5m2": (ml_dtypes.float8_e5m2, 14)}[fmt]
    v = np.moveaxis(np.asarray(x, np.float32).astype(ml_dtypes.bfloat16).astype(np.float64), axis, -1)
    blocks = v.reshape(v.shape[:-1] + (-1, 32))
    amax = np.abs(blocks).max(-1, keepdims=True)
    byte = np.maximum(np.where(amax > 0, np.frexp(amax)[1] - 1 + 127, 0) - down, 1)
    scale = np.exp2(byte - 127.0)
    codes = (blocks / scale).astype(np.float32).astype(dtype).astype(np.float64)
    return np.moveaxis((codes * scale).reshape(v.shape), -1, axis)


WIDE = False


def mx_kscale(k):
    if not WIDE:
        return np.ones(k)
    levels = np.array([30, -30])
    if k % 512:
        return np.exp2(np.random.permutation(np.resize(levels, k // 32))).repeat(32)
    a = np.empty((k // 512, 16))
    for p in range(k // 512):
        a[p, :8] = np.random.permutation(np.resize(levels, 8))
        for g in range(8):
            far = levels[np.abs(levels - a[p, g]) >= 10]
            a[p, g + 8] = far[np.random.randint(len(far))]
    return np.exp2(a.ravel()).repeat(32)


def f64(x):
    return np.asarray(x).astype(np.float64)


E2M1 = np.array([0.0, 0.5, 1.0, 1.5, 2.0, 3.0, 4.0, 6.0, -0.0, -0.5, -1.0, -1.5, -2.0, -3.0, -4.0, -6.0])


def pack_weight(w, fmt):
    k, n = w.shape
    w = f64(np.asarray(w, np.float32).astype(ml_dtypes.bfloat16)).reshape(k // 32, 32, n)
    amax = np.abs(w).max(1)
    if fmt == "e4m3":
        byte = np.frexp(amax)[1] - 1 + 127 - 7
    else:
        mant, ex = np.frexp(amax / 6.0)
        byte = np.where(mant > 0.5, ex, ex - 1) + 127
    byte = np.clip(np.where(amax > 0, byte, 1), 1, 254)
    scaled = (w * np.exp2(127.0 - byte)[:, None, :]).reshape(k, n).astype(np.float32)
    by_word = np.ascontiguousarray(scaled.reshape(k // 512, 128, 4, n).transpose(0, 1, 3, 2))
    if fmt == "e4m3":
        words = by_word.astype(ml_dtypes.float8_e4m3fn).view(np.uint8)
    else:
        c = by_word.astype(ml_dtypes.float4_e2m1fn).view(np.uint8) & 0xF
        words = (c[..., 0::2] | (c[..., 1::2] << 4)).reshape(k // 512, 128, 2 * n)
    return np.ascontiguousarray(words), np.ascontiguousarray(byte.astype(np.uint8).reshape(k // 512, 16, n))


def unpack_weight(words, scales, fmt):
    g, _, n = scales.shape
    words = np.ascontiguousarray(words).reshape(g, 128, n, -1)
    if fmt == "e4m3":
        vals = words.view(ml_dtypes.float8_e4m3fn).astype(np.float64)
    else:
        nib = np.empty((g, 128, n, 4), np.uint8)
        nib[..., 0::2] = words & 0xF
        nib[..., 1::2] = words >> 4
        vals = E2M1[nib]
    vals = vals * np.repeat(np.exp2(scales.astype(np.float64) - 127.0), 8, axis=1)[..., None]
    return vals.transpose(0, 1, 3, 2).reshape(g * 512, n)


O, K, M, T = 1024, 1536, 512, 1024


def setup_inputs():
    n = np.random.standard_normal
    s = mx_kscale(K)[:, None]
    dy = np.exp(0.5 * n((1, T))) * n((K, T))
    w = n((K, M)) / np.sqrt(K) / s
    p_w8 = pack_weight(w[:O], "e4m3")
    p_w4 = pack_weight(w[O:], "e2m1")
    return {
        "dy": (dy * s).astype(np.float32),
        "w8_words": p_w8[0],
        "w8_scales": p_w8[1],
        "w4_words": p_w4[0],
        "w4_scales": p_w4[1],
        "r": (n((512, 1024))).astype(np.float32),
    }


def reference(dy, w8_words, w8_scales, w4_words, w4_scales, r):
    dy_ = mxq(f64(dy), 0, "e5m2")
    w8_ = unpack_weight(w8_words, w8_scales, "e4m3")
    w4_ = unpack_weight(w4_words, w4_scales, "e2m1")
    y = w8_.T @ dy_[:O] + w4_.T @ dy_[O:]
    return f64(r) + y

@@ -1,0 +1,130 @@
+from contextlib import ExitStack
+
+import concourse.mybir as mybir
+
+O, K, M, T = 1024, 1536, 512, 1024
+FLOPS = 2 * K * M * T
+
+F32 = mybir.dt.float32
+BF16 = mybir.dt.bfloat16
+I32 = mybir.dt.int32
+U32 = mybir.dt.uint32
+U8 = mybir.dt.uint8
+E4M3X4 = mybir.dt.float8_e4m3fn_x4
+E5M2X4 = mybir.dt.float8_e5m2_x4
+E2M1X4 = mybir.dt.float4_e2m1fn_x4
+
+P = 128
+PACK = 4
+K_PASS = P * PACK
+N_TILE = 512
+HALVES = T // N_TILE
+D_TILES = M // P
+QUADRANTS = 4
+QUADRANT = 32
+PASS_ORDER = (2, 0, 1)
+VECTOR_A = slice(0, 256)
+VECTOR_B = slice(256, 384)
+SCALAR_C = slice(384, 512)
+
+
+def tile_mix_dyq_fm_res_kernel(tc, dy, w8_words, w8_scales, w4_words, w4_scales, r, out):
+    nc = tc.nc
+    with ExitStack() as ctx:
+        keep = ctx.enter_context(tc.tile_pool(name="keep", bufs=1))
+        psum = ctx.enter_context(tc.psum_pool(name="psum", bufs=1))
+        ctx.enter_context(tc.manual_schedule())
+
+        w8_scale = keep.tile([P, 2, M], U8, align_bytes=64)
+        w4_scale = keep.tile([P, M], U8, align_bytes=64)
+        warm_in = keep.tile([P, 8], F32)
+        warm_out = keep.tile([P, 8], F32)
+        nc.vector.memset(w4_scale[:].bitcast(I32), 0)
+        nc.vector.memset(w8_scale[:].rearrange("p a d -> p (a d)").bitcast(I32), 0)
+        nc.vector.memset(warm_in[:], 0.0)
+        nc.scalar.copy(out=warm_out[:], in_=warm_in[:])
+        for q in range(QUADRANTS):
+            nc.gpsimd.dma_start(
+                out=w4_scale[QUADRANT * q : QUADRANT * q + 4, :].bitcast(I32),
+                in_=w4_scales[0, 4 * q : 4 * q + 4, :].bitcast(I32),
+            )
+        for q in range(QUADRANTS):
+            nc.gpsimd.dma_start(
+                out=w8_scale[QUADRANT * q : QUADRANT * q + 4, :, :].bitcast(I32),
+                in_=w8_scales[:, 4 * q : 4 * q + 4, :].rearrange("a s d -> s a d").bitcast(I32),
+            )
+
+        w8 = [keep.tile([P, M], U32, align_bytes=64, name=f"w8_{a}") for a in range(2)]
+        w4 = keep.tile([P, 2 * M], U8, align_bytes=64)
+        raw = {}
+        for g in PASS_ORDER:
+            rows = dy[g * K_PASS : (g + 1) * K_PASS, :].rearrange("(p j) t -> p j t", j=PACK)
+            if g != PASS_ORDER[-1]:
+                whole = keep.tile([P, PACK, T], F32, name=f"raw_{g}")
+                nc.sync.dma_start(out=whole[:], in_=rows)
+                for h in range(HALVES):
+                    raw[g, h] = whole[:, :, h * N_TILE : (h + 1) * N_TILE]
+            else:
+                for h in range(HALVES):
+                    half = keep.tile([P, PACK, N_TILE], F32, name=f"raw_{g}_{h}")
+                    nc.sync.dma_start(out=half[:], in_=rows[:, :, h * N_TILE : (h + 1) * N_TILE])
+                    raw[g, h] = half[:]
+            if g < 2:
+                nc.sync.dma_start(
+                    out=w8[g][:].bitcast(I32),
+                    in_=w8_words[g].rearrange("p d i -> p (d i)").bitcast(I32),
+                )
+            else:
+                nc.sync.dma_start(out=w4[:].bitcast(I32), in_=w4_words[0].bitcast(I32))
+        res = []
+        for m in range(D_TILES):
+            r_tile = keep.tile([P, T], F32, name=f"r_{m}")
+            nc.sync.dma_start(out=r_tile[:], in_=r[m * P : (m + 1) * P, :])
+            res.append(r_tile)
+
+        acc = {}
+        for m in range(D_TILES):
+            for h in range(HALVES):
+                acc[m, h] = psum.tile([P, N_TILE], F32, name=f"acc_{m}_{h}")
+
+        for g in PASS_ORDER:
+            for h in range(HALVES):
+                src = raw[g, h].rearrange("p j t -> p t j")
+                grouped = keep.tile([P, N_TILE, PACK], BF16, align_bytes=64, name=f"grouped_{g}_{h}")
+                codes = keep.tile([P, N_TILE], U32, align_bytes=64, name=f"codes_{g}_{h}")
+                scale = keep.tile([P, N_TILE], U8, align_bytes=64, name=f"scale_{g}_{h}")
+                nc.scalar.copy(out=grouped[:, SCALAR_C, :], in_=src[:, SCALAR_C, :])
+                nc.vector.tensor_copy(out=grouped[:, VECTOR_A, :], in_=src[:, VECTOR_A, :])
+                nc.vector.tensor_copy(out=grouped[:, VECTOR_B, :], in_=src[:, VECTOR_B, :])
+                for cols in (slice(0, 256), slice(256, 512)):
+                    nc.vector.quantize_mx(
+                        out=codes[:, cols].bitcast(E5M2X4),
+                        scales=scale[:, cols],
+                        in_=grouped[:, cols, :].rearrange("p t j -> p (t j)"),
+                    )
+                for m in range(D_TILES):
+                    d_cols = slice(m * P, (m + 1) * P)
+                    if g < 2:
+                        lhsT = w8[g][:, d_cols].bitcast(E4M3X4)
+                        lhsT_scale = w8_scale[:, g, d_cols]
+                    else:
+                        lhsT = w4[:, 2 * m * P : 2 * (m + 1) * P].bitcast(E2M1X4)
+                        lhsT_scale = w4_scale[:, d_cols]
+                    nc.tensor.matmul_mx(
+                        out=acc[m, h][:],
+                        lhsT=lhsT,
+                        lhsT_scale=lhsT_scale,
+                        rhs=codes[:].bitcast(E5M2X4),
+                        rhs_scale=scale[:],
+                        start=(g == PASS_ORDER[0]),
+                        stop=(g == PASS_ORDER[-1]),
+                    )
+
+        for m in range(D_TILES):
+            total = keep.tile([P, T], F32, name=f"total_{m}")
+            for h in range(HALVES):
+                t_cols = slice(h * N_TILE, (h + 1) * N_TILE)
+                nc.vector.tensor_tensor(
+                    out=total[:, t_cols], in0=acc[m, h][:], in1=res[m][:, t_cols], op=mybir.AluOpType.add
+                )
+            nc.sync.dma_start(out=out[m * P : (m + 1) * P, :], in_=total[:])

@@ -22,10 +22,10 @@ HALVES = T // N_TILE
 D_TILES = M // P
 QUADRANTS = 4
 QUADRANT = 32
-PASS_ORDER = (2, 0, 1)
-VECTOR_A = slice(0, 256)
-VECTOR_B = slice(256, 384)
-SCALAR_C = slice(384, 512)
+QUARTER = 256
+LINE = 4
+LAST = 1
+LATE_TOKENS = 256
 
 
 def tile_mix_dyq_fm_res_kernel(tc, dy, w8_words, w8_scales, w4_words, w4_scales, r, out):
@@ -37,89 +37,124 @@ def tile_mix_dyq_fm_res_kernel(tc, dy, w8_words, w8_scales, w4_words, w4_scales,
 
         w8_scale = keep.tile([P, 2, M], U8, align_bytes=64)
         w4_scale = keep.tile([P, M], U8, align_bytes=64)
-        warm_in = keep.tile([P, 8], F32)
-        warm_out = keep.tile([P, 8], F32)
         nc.vector.memset(w4_scale[:].bitcast(I32), 0)
         nc.vector.memset(w8_scale[:].rearrange("p a d -> p (a d)").bitcast(I32), 0)
-        nc.vector.memset(warm_in[:], 0.0)
-        nc.scalar.copy(out=warm_out[:], in_=warm_in[:])
-        for q in range(QUADRANTS):
-            nc.gpsimd.dma_start(
-                out=w4_scale[QUADRANT * q : QUADRANT * q + 4, :].bitcast(I32),
-                in_=w4_scales[0, 4 * q : 4 * q + 4, :].bitcast(I32),
-            )
-        for q in range(QUADRANTS):
-            nc.gpsimd.dma_start(
-                out=w8_scale[QUADRANT * q : QUADRANT * q + 4, :, :].bitcast(I32),
-                in_=w8_scales[:, 4 * q : 4 * q + 4, :].rearrange("a s d -> s a d").bitcast(I32),
-            )
 
         w8 = [keep.tile([P, M], U32, align_bytes=64, name=f"w8_{a}") for a in range(2)]
         w4 = keep.tile([P, 2 * M], U8, align_bytes=64)
+        res = [keep.tile([P, T], F32, name=f"r_{m}") for m in range(D_TILES)]
         raw = {}
-        for g in PASS_ORDER:
+
+        def load_dy(g, t0, t1):
             rows = dy[g * K_PASS : (g + 1) * K_PASS, :].rearrange("(p j) t -> p j t", j=PACK)
-            if g != PASS_ORDER[-1]:
-                whole = keep.tile([P, PACK, T], F32, name=f"raw_{g}")
-                nc.sync.dma_start(out=whole[:], in_=rows)
-                for h in range(HALVES):
-                    raw[g, h] = whole[:, :, h * N_TILE : (h + 1) * N_TILE]
-            else:
-                for h in range(HALVES):
-                    half = keep.tile([P, PACK, N_TILE], F32, name=f"raw_{g}_{h}")
-                    nc.sync.dma_start(out=half[:], in_=rows[:, :, h * N_TILE : (h + 1) * N_TILE])
-                    raw[g, h] = half[:]
-            if g < 2:
-                nc.sync.dma_start(
-                    out=w8[g][:].bitcast(I32),
-                    in_=w8_words[g].rearrange("p d i -> p (d i)").bitcast(I32),
-                )
-            else:
-                nc.sync.dma_start(out=w4[:].bitcast(I32), in_=w4_words[0].bitcast(I32))
-        res = []
+            raw[g, t0] = keep.tile([P, PACK, t1 - t0], F32, name=f"raw_{g}_{t0}")
+            nc.sync.dma_start(out=raw[g, t0][:], in_=rows[:, :, t0:t1])
+
+        def load_w8(a):
+            nc.sync.dma_start(
+                out=w8[a][:].bitcast(I32),
+                in_=w8_words[a].rearrange("p d i -> p (d i)").bitcast(I32),
+            )
+
+        def load_w4_scale(s):
+            nc.sync.dma_start(
+                out=w4_scale[s:P:QUADRANT, :].bitcast(I32),
+                in_=w4_scales[0, s:16:4, :].bitcast(I32),
+            )
+
+        def load_w8_scale(s):
+            nc.sync.dma_start(
+                out=w8_scale[s:P:QUADRANT, :, :].bitcast(I32),
+                in_=w8_scales[:, s:16:4, :].rearrange("a q d -> q a d").bitcast(I32),
+            )
+
+        load_dy(2, 0, T)
+        for s in range(4):
+            load_w4_scale(s)
+        nc.sync.dma_start(out=w4[:].bitcast(I32), in_=w4_words[0].bitcast(I32))
+        load_dy(0, 0, T)
+        for s in range(4):
+            load_w8_scale(s)
+        load_w8(0)
+        load_dy(LAST, 0, T - LATE_TOKENS)
+        load_dy(LAST, T - LATE_TOKENS, T)
+        load_w8(1)
         for m in range(D_TILES):
-            r_tile = keep.tile([P, T], F32, name=f"r_{m}")
-            nc.sync.dma_start(out=r_tile[:], in_=r[m * P : (m + 1) * P, :])
-            res.append(r_tile)
+            nc.sync.dma_start(out=res[m][:], in_=r[m * P : (m + 1) * P, :])
 
         acc = {}
         for m in range(D_TILES):
             for h in range(HALVES):
                 acc[m, h] = psum.tile([P, N_TILE], F32, name=f"acc_{m}_{h}")
 
-        for g in PASS_ORDER:
+        codes = {}
+        scale = {}
+        for g in range(3):
             for h in range(HALVES):
-                src = raw[g, h].rearrange("p j t -> p t j")
-                grouped = keep.tile([P, N_TILE, PACK], BF16, align_bytes=64, name=f"grouped_{g}_{h}")
-                codes = keep.tile([P, N_TILE], U32, align_bytes=64, name=f"codes_{g}_{h}")
-                scale = keep.tile([P, N_TILE], U8, align_bytes=64, name=f"scale_{g}_{h}")
-                nc.scalar.copy(out=grouped[:, SCALAR_C, :], in_=src[:, SCALAR_C, :])
-                nc.vector.tensor_copy(out=grouped[:, VECTOR_A, :], in_=src[:, VECTOR_A, :])
-                nc.vector.tensor_copy(out=grouped[:, VECTOR_B, :], in_=src[:, VECTOR_B, :])
-                for cols in (slice(0, 256), slice(256, 512)):
-                    nc.vector.quantize_mx(
-                        out=codes[:, cols].bitcast(E5M2X4),
-                        scales=scale[:, cols],
-                        in_=grouped[:, cols, :].rearrange("p t j -> p (t j)"),
-                    )
-                for m in range(D_TILES):
-                    d_cols = slice(m * P, (m + 1) * P)
-                    if g < 2:
-                        lhsT = w8[g][:, d_cols].bitcast(E4M3X4)
-                        lhsT_scale = w8_scale[:, g, d_cols]
-                    else:
-                        lhsT = w4[:, 2 * m * P : 2 * (m + 1) * P].bitcast(E2M1X4)
-                        lhsT_scale = w4_scale[:, d_cols]
-                    nc.tensor.matmul_mx(
-                        out=acc[m, h][:],
-                        lhsT=lhsT,
-                        lhsT_scale=lhsT_scale,
-                        rhs=codes[:].bitcast(E5M2X4),
-                        rhs_scale=scale[:],
-                        start=(g == PASS_ORDER[0]),
-                        stop=(g == PASS_ORDER[-1]),
-                    )
+                codes[g, h] = keep.tile([P, N_TILE], U32, align_bytes=64, name=f"codes_{g}_{h}")
+                scale[g, h] = keep.tile([P, N_TILE], U8, align_bytes=64, name=f"scale_{g}_{h}")
+        grouped = {}
 
+        def interleave(engine, g, base, t0, t1):
+            grouped[g, t0] = keep.tile([P, t1 - t0, PACK], BF16, align_bytes=64, name=f"grouped_{g}_{t0}")
+            src = raw[g, base][:, :, t0 - base : t1 - base].rearrange("p j (c i) -> p c j i", i=LINE)
+            dst = grouped[g, t0][:].rearrange("p (c i) j -> p c j i", i=LINE)
+            if engine == "vector":
+                nc.vector.tensor_copy(out=dst, in_=src)
+            else:
+                nc.scalar.copy(out=dst, in_=src)
+
+        def quantise(g, t0, t1):
+            h = t0 // N_TILE
+            cols = slice(t0 - h * N_TILE, t1 - h * N_TILE)
+            nc.vector.quantize_mx(
+                out=codes[g, h][:, cols].bitcast(E5M2X4),
+                scales=scale[g, h][:, cols],
+                in_=grouped[g, t0][:].rearrange("p t j -> p (t j)"),
+            )
+
+        def multiply(g, m, h, start):
+            d_cols = slice(m * P, (m + 1) * P)
+            if g < 2:
+                lhsT = w8[g][:, d_cols].bitcast(E4M3X4)
+                lhsT_scale = w8_scale[:, g, d_cols]
+            else:
+                lhsT = w4[:, 2 * m * P : 2 * (m + 1) * P].bitcast(E2M1X4)
+                lhsT_scale = w4_scale[:, d_cols]
+            nc.tensor.matmul_mx(
+                out=acc[m, h][:],
+                lhsT=lhsT,
+                lhsT_scale=lhsT_scale,
+                rhs=codes[g, h][:].bitcast(E5M2X4),
+                rhs_scale=scale[g, h][:],
+                start=start,
+                stop=(g == LAST),
+            )
+
+        for g in (2, 0):
+            for u in range(4):
+                interleave(("vector", "scalar")[u % 2], g, 0, u * QUARTER, (u + 1) * QUARTER)
+            for u in range(4):
+                quantise(g, u * QUARTER, (u + 1) * QUARTER)
+        for g, h, start in ((2, 0, True), (0, 0, False), (0, 1, True), (2, 1, False)):
+            for m in range(D_TILES):
+                multiply(g, m, h, start)
+
+        late = T - LATE_TOKENS
+        mid = late + LATE_TOKENS // 2
+        interleave("vector", LAST, 0, 0, QUARTER)
+        interleave("scalar", LAST, 0, QUARTER, 2 * QUARTER)
+        interleave("vector", LAST, 0, 2 * QUARTER, late)
+        interleave("scalar", LAST, late, mid, T)
+        quantise(LAST, 0, QUARTER)
+        quantise(LAST, QUARTER, 2 * QUARTER)
+        interleave("vector", LAST, late, late, mid)
+        quantise(LAST, 2 * QUARTER, late)
+        quantise(LAST, late, mid)
+        quantise(LAST, mid, T)
+
+        for m, h in ((0, 0), (1, 0), (0, 1), (1, 1), (2, 0), (2, 1), (3, 0), (3, 1)):
+            multiply(LAST, m, h, False)
         for m in range(D_TILES):
             total = keep.tile([P, T], F32, name=f"total_{m}")
             for h in range(HALVES):

@@ -25,7 +25,7 @@ QUADRANT = 32
 QUARTER = 256
 LINE = 4
 LAST = 1
-LATE_TOKENS = 256
+PAIR = 2
 
 
 def tile_mix_dyq_fm_res_kernel(tc, dy, w8_words, w8_scales, w4_words, w4_scales, r, out):
@@ -45,10 +45,10 @@ def tile_mix_dyq_fm_res_kernel(tc, dy, w8_words, w8_scales, w4_words, w4_scales,
         res = [keep.tile([P, T], F32, name=f"r_{m}") for m in range(D_TILES)]
         raw = {}
 
-        def load_dy(g, t0, t1):
+        def load_dy(g, j0, j1):
             rows = dy[g * K_PASS : (g + 1) * K_PASS, :].rearrange("(p j) t -> p j t", j=PACK)
-            raw[g, t0] = keep.tile([P, PACK, t1 - t0], F32, name=f"raw_{g}_{t0}")
-            nc.sync.dma_start(out=raw[g, t0][:], in_=rows[:, :, t0:t1])
+            raw[g, j0] = keep.tile([P, j1 - j0, T], F32, name=f"raw_{g}_{j0}")
+            nc.sync.dma_start(out=raw[g, j0][:], in_=rows[:, j0:j1, :])
 
         def load_w8(a):
             nc.sync.dma_start(
@@ -68,16 +68,16 @@ def tile_mix_dyq_fm_res_kernel(tc, dy, w8_words, w8_scales, w4_words, w4_scales,
                 in_=w8_scales[:, s:16:4, :].rearrange("a q d -> q a d").bitcast(I32),
             )
 
-        load_dy(2, 0, T)
+        load_dy(2, 0, PACK)
         for s in range(4):
             load_w4_scale(s)
-        nc.sync.dma_start(out=w4[:].bitcast(I32), in_=w4_words[0].bitcast(I32))
-        load_dy(0, 0, T)
+        load_dy(0, 0, PACK)
         for s in range(4):
             load_w8_scale(s)
+        nc.sync.dma_start(out=w4[:].bitcast(I32), in_=w4_words[0].bitcast(I32))
+        load_dy(LAST, 0, PAIR)
+        load_dy(LAST, PAIR, PACK)
         load_w8(0)
-        load_dy(LAST, 0, T - LATE_TOKENS)
-        load_dy(LAST, T - LATE_TOKENS, T)
         load_w8(1)
         for m in range(D_TILES):
             nc.sync.dma_start(out=res[m][:], in_=r[m * P : (m + 1) * P, :])
@@ -94,15 +94,24 @@ def tile_mix_dyq_fm_res_kernel(tc, dy, w8_words, w8_scales, w4_words, w4_scales,
                 codes[g, h] = keep.tile([P, N_TILE], U32, align_bytes=64, name=f"codes_{g}_{h}")
                 scale[g, h] = keep.tile([P, N_TILE], U8, align_bytes=64, name=f"scale_{g}_{h}")
         grouped = {}
+        for g in range(3):
+            for u in range(4):
+                grouped[g, u * QUARTER] = keep.tile([P, QUARTER, PACK], BF16, align_bytes=64, name=f"grouped_{g}_{u}")
 
-        def interleave(engine, g, base, t0, t1):
-            grouped[g, t0] = keep.tile([P, t1 - t0, PACK], BF16, align_bytes=64, name=f"grouped_{g}_{t0}")
-            src = raw[g, base][:, :, t0 - base : t1 - base].rearrange("p j (c i) -> p c j i", i=LINE)
-            dst = grouped[g, t0][:].rearrange("p (c i) j -> p c j i", i=LINE)
-            if engine == "vector":
-                nc.vector.tensor_copy(out=dst, in_=src)
-            else:
-                nc.scalar.copy(out=dst, in_=src)
+        def interleave(g, j0, j1):
+            for u in range(4):
+                t0 = u * QUARTER
+                src = raw[g, j0][:, :, t0 : t0 + QUARTER]
+                dst = grouped[g, t0][:, :, j0:j1]
+                if j1 - j0 == PACK:
+                    src = src.rearrange("p j (c i) -> p c j i", i=LINE)
+                    dst = dst.rearrange("p (c i) j -> p c j i", i=LINE)
+                else:
+                    src = src.rearrange("p j t -> p t j")
+                if u % 2 == 0:
+                    nc.vector.tensor_copy(out=dst, in_=src)
+                else:
+                    nc.scalar.copy(out=dst, in_=src)
 
         def quantise(g, t0, t1):
             h = t0 // N_TILE
@@ -113,7 +122,7 @@ def tile_mix_dyq_fm_res_kernel(tc, dy, w8_words, w8_scales, w4_words, w4_scales,
                 in_=grouped[g, t0][:].rearrange("p t j -> p (t j)"),
             )
 
-        def multiply(g, m, h, start):
+        def multiply(g, m, h):
             d_cols = slice(m * P, (m + 1) * P)
             if g < 2:
                 lhsT = w8[g][:, d_cols].bitcast(E4M3X4)
@@ -127,34 +136,28 @@ def tile_mix_dyq_fm_res_kernel(tc, dy, w8_words, w8_scales, w4_words, w4_scales,
                 lhsT_scale=lhsT_scale,
                 rhs=codes[g, h][:].bitcast(E5M2X4),
                 rhs_scale=scale[g, h][:],
-                start=start,
+                start=(g == 2),
                 stop=(g == LAST),
             )
 
         for g in (2, 0):
-            for u in range(4):
-                interleave(("vector", "scalar")[u % 2], g, 0, u * QUARTER, (u + 1) * QUARTER)
+            interleave(g, 0, PACK)
             for u in range(4):
                 quantise(g, u * QUARTER, (u + 1) * QUARTER)
-        for g, h, start in ((2, 0, True), (0, 0, False), (0, 1, True), (2, 1, False)):
+        for h in range(HALVES):
             for m in range(D_TILES):
-                multiply(g, m, h, start)
+                multiply(2, m, h)
 
-        late = T - LATE_TOKENS
-        mid = late + LATE_TOKENS // 2
-        interleave("vector", LAST, 0, 0, QUARTER)
-        interleave("scalar", LAST, 0, QUARTER, 2 * QUARTER)
-        interleave("vector", LAST, 0, 2 * QUARTER, late)
-        interleave("scalar", LAST, late, mid, T)
-        quantise(LAST, 0, QUARTER)
-        quantise(LAST, QUARTER, 2 * QUARTER)
-        interleave("vector", LAST, late, late, mid)
-        quantise(LAST, 2 * QUARTER, late)
-        quantise(LAST, late, mid)
-        quantise(LAST, mid, T)
+        interleave(LAST, 0, PAIR)
+        interleave(LAST, PAIR, PACK)
+        for u in range(4):
+            quantise(LAST, u * QUARTER, (u + 1) * QUARTER)
 
-        for m, h in ((0, 0), (1, 0), (0, 1), (1, 1), (2, 0), (2, 1), (3, 0), (3, 1)):
-            multiply(LAST, m, h, False)
+        for m0 in range(0, D_TILES, 2):
+            for g in (0, LAST):
+                for h in range(HALVES):
+                    for m in (m0, m0 + 1):
+                        multiply(g, m, h)
         for m in range(D_TILES):
             total = keep.tile([P, T], F32, name=f"total_{m}")
             for h in range(HALVES):

@@ -26,6 +26,7 @@ QUARTER = 256
 LINE = 4
 LAST = 1
 PAIR = 2
+POOL_COLS = 256
 
 
 def tile_mix_dyq_fm_res_kernel(tc, dy, w8_words, w8_scales, w4_words, w4_scales, r, out):
@@ -72,11 +73,11 @@ def tile_mix_dyq_fm_res_kernel(tc, dy, w8_words, w8_scales, w4_words, w4_scales,
         for s in range(4):
             load_w4_scale(s)
         load_dy(0, 0, PACK)
-        for s in range(4):
-            load_w8_scale(s)
         nc.sync.dma_start(out=w4[:].bitcast(I32), in_=w4_words[0].bitcast(I32))
         load_dy(LAST, 0, PAIR)
         load_dy(LAST, PAIR, PACK)
+        for s in range(4):
+            load_w8_scale(s)
         load_w8(0)
         load_w8(1)
         for m in range(D_TILES):
@@ -153,16 +154,30 @@ def tile_mix_dyq_fm_res_kernel(tc, dy, w8_words, w8_scales, w4_words, w4_scales,
         for u in range(4):
             quantise(LAST, u * QUARTER, (u + 1) * QUARTER)
 
-        for m0 in range(0, D_TILES, 2):
-            for g in (0, LAST):
-                for h in range(HALVES):
-                    for m in (m0, m0 + 1):
-                        multiply(g, m, h)
+        for g in (0, LAST):
+            for h in range(HALVES):
+                for m in (0, 1):
+                    multiply(g, m, h)
+        for m in (2, 3):
+            for h in range(HALVES):
+                for g in (0, LAST):
+                    multiply(g, m, h)
         for m in range(D_TILES):
             total = keep.tile([P, T], F32, name=f"total_{m}")
-            for h in range(HALVES):
-                t_cols = slice(h * N_TILE, (h + 1) * N_TILE)
-                nc.vector.tensor_tensor(
-                    out=total[:, t_cols], in0=acc[m, h][:], in1=res[m][:, t_cols], op=mybir.AluOpType.add
+            first = POOL_COLS if m > 0 else 0
+            if first:
+                drained = keep.tile([P, first], F32, name=f"drained_{m}")
+                nc.scalar.copy(out=drained[:], in_=acc[m, 0][:, :first])
+                nc.gpsimd.tensor_tensor(
+                    out=total[:, :first], in0=drained[:], in1=res[m][:, :first], op=mybir.AluOpType.add
                 )
+            nc.vector.tensor_tensor(
+                out=total[:, first:N_TILE],
+                in0=acc[m, 0][:, first:],
+                in1=res[m][:, first:N_TILE],
+                op=mybir.AluOpType.add,
+            )
+            nc.vector.tensor_tensor(
+                out=total[:, N_TILE:], in0=acc[m, 1][:], in1=res[m][:, N_TILE:], op=mybir.AluOpType.add
+            )
             nc.sync.dma_start(out=out[m * P : (m + 1) * P, :], in_=total[:])

@@ -36,19 +36,19 @@ def tile_mix_dyq_fm_res_kernel(tc, dy, w8_words, w8_scales, w4_words, w4_scales,
         psum = ctx.enter_context(tc.psum_pool(name="psum", bufs=1))
         ctx.enter_context(tc.manual_schedule())
 
-        w8_scale = keep.tile([P, 2, M], U8, align_bytes=64)
-        w4_scale = keep.tile([P, M], U8, align_bytes=64)
+        w8_scale = keep.tile([P, 2, M], U8, align_bytes=256)
+        w4_scale = keep.tile([P, M], U8, align_bytes=256)
         nc.vector.memset(w4_scale[:].bitcast(I32), 0)
         nc.vector.memset(w8_scale[:].rearrange("p a d -> p (a d)").bitcast(I32), 0)
 
-        w8 = [keep.tile([P, M], U32, align_bytes=64, name=f"w8_{a}") for a in range(2)]
-        w4 = keep.tile([P, 2 * M], U8, align_bytes=64)
-        res = [keep.tile([P, T], F32, name=f"r_{m}") for m in range(D_TILES)]
+        w8 = [keep.tile([P, M], U32, align_bytes=256, name=f"w8_{a}") for a in range(2)]
+        w4 = keep.tile([P, 2 * M], U8, align_bytes=256)
+        res = [keep.tile([P, T], F32, align_bytes=256, name=f"r_{m}") for m in range(D_TILES)]
         raw = {}
 
         def load_dy(g, j0, j1):
             rows = dy[g * K_PASS : (g + 1) * K_PASS, :].rearrange("(p j) t -> p j t", j=PACK)
-            raw[g, j0] = keep.tile([P, j1 - j0, T], F32, name=f"raw_{g}_{j0}")
+            raw[g, j0] = keep.tile([P, j1 - j0, T], F32, align_bytes=256, name=f"raw_{g}_{j0}")
             nc.sync.dma_start(out=raw[g, j0][:], in_=rows[:, j0:j1, :])
 
         def load_w8(a):
@@ -163,7 +163,7 @@ def tile_mix_dyq_fm_res_kernel(tc, dy, w8_words, w8_scales, w4_words, w4_scales,
                 for g in (0, LAST):
                     multiply(g, m, h)
         for m in range(D_TILES):
-            total = keep.tile([P, T], F32, name=f"total_{m}")
+            total = keep.tile([P, T], F32, align_bytes=256, name=f"total_{m}")
             first = POOL_COLS if m > 0 else 0
             if first:
                 drained = keep.tile([P, first], F32, name=f"drained_{m}")

@@ -177,7 +177,12 @@ def tile_mix_dyq_fm_res_kernel(tc, dy, w8_words, w8_scales, w4_words, w4_scales,
                 in1=res[m][:, first:N_TILE],
                 op=mybir.AluOpType.add,
             )
+            if m == 0:
+                nc.sync.dma_start(out=out[:P, :N_TILE], in_=total[:, :N_TILE])
             nc.vector.tensor_tensor(
                 out=total[:, N_TILE:], in0=acc[m, 1][:], in1=res[m][:, N_TILE:], op=mybir.AluOpType.add
             )
-            nc.sync.dma_start(out=out[m * P : (m + 1) * P, :], in_=total[:])
+            if m == 0:
+                nc.sync.dma_start(out=out[:P, N_TILE:], in_=total[:, N_TILE:])
+            else:
+                nc.sync.dma_start(out=out[m * P : (m + 1) * P, :], in_=total[:])

@@ -20,13 +20,12 @@ K_PASS = P * PACK
 N_TILE = 512
 HALVES = T // N_TILE
 D_TILES = M // P
-QUADRANTS = 4
 QUADRANT = 32
 QUARTER = 256
 LINE = 4
 LAST = 1
 PAIR = 2
-POOL_COLS = 256
+POOL_COLS = 160
 
 
 def tile_mix_dyq_fm_res_kernel(tc, dy, w8_words, w8_scales, w4_words, w4_scales, r, out):
@@ -46,10 +45,12 @@ def tile_mix_dyq_fm_res_kernel(tc, dy, w8_words, w8_scales, w4_words, w4_scales,
         res = [keep.tile([P, T], F32, align_bytes=256, name=f"r_{m}") for m in range(D_TILES)]
         raw = {}
 
-        def load_dy(g, j0, j1):
+        def load_dy(g, j0, j1, t0, t1):
             rows = dy[g * K_PASS : (g + 1) * K_PASS, :].rearrange("(p j) t -> p j t", j=PACK)
-            raw[g, j0] = keep.tile([P, j1 - j0, T], F32, align_bytes=256, name=f"raw_{g}_{j0}")
-            nc.sync.dma_start(out=raw[g, j0][:], in_=rows[:, j0:j1, :])
+            piece = keep.tile([P, j1 - j0, t1 - t0], F32, align_bytes=256, name=f"raw_{g}_{j0}_{t0}")
+            for u in range(t0 // QUARTER, t1 // QUARTER):
+                raw[g, j0, u] = piece[:, :, u * QUARTER - t0 : (u + 1) * QUARTER - t0]
+            nc.sync.dma_start(out=piece[:], in_=rows[:, j0:j1, t0:t1])
 
         def load_w8(a):
             nc.sync.dma_start(
@@ -63,21 +64,28 @@ def tile_mix_dyq_fm_res_kernel(tc, dy, w8_words, w8_scales, w4_words, w4_scales,
                 in_=w4_scales[0, s:16:4, :].bitcast(I32),
             )
 
-        def load_w8_scale(s):
+        def load_w8_scale(a, s):
             nc.sync.dma_start(
-                out=w8_scale[s:P:QUADRANT, :, :].bitcast(I32),
-                in_=w8_scales[:, s:16:4, :].rearrange("a q d -> q a d").bitcast(I32),
+                out=w8_scale[s:P:QUADRANT, a, :].bitcast(I32),
+                in_=w8_scales[a, s:16:4, :].bitcast(I32),
             )
 
-        load_dy(2, 0, PACK)
-        for s in range(4):
+        load_dy(2, 0, PACK, 0, T)
+        for s in range(3):
             load_w4_scale(s)
-        load_dy(0, 0, PACK)
+        for q in range(2):
+            nc.sync.dma_start(
+                out=w4_scale[q * QUADRANT + 3 : P : 2 * QUADRANT, :].bitcast(I32),
+                in_=w4_scales[0, 4 * q + 3 : 16 : 8, :].bitcast(I32),
+            )
+        load_dy(0, 0, PACK, 0, T)
         nc.sync.dma_start(out=w4[:].bitcast(I32), in_=w4_words[0].bitcast(I32))
-        load_dy(LAST, 0, PAIR)
-        load_dy(LAST, PAIR, PACK)
+        load_dy(LAST, 0, PAIR, 0, T)
         for s in range(4):
-            load_w8_scale(s)
+            load_w8_scale(0, s)
+        load_dy(LAST, PAIR, PACK, 0, T)
+        for s in range(4):
+            load_w8_scale(1, s)
         load_w8(0)
         load_w8(1)
         for m in range(D_TILES):
@@ -97,30 +105,28 @@ def tile_mix_dyq_fm_res_kernel(tc, dy, w8_words, w8_scales, w4_words, w4_scales,
         grouped = {}
         for g in range(3):
             for u in range(4):
-                grouped[g, u * QUARTER] = keep.tile([P, QUARTER, PACK], BF16, align_bytes=64, name=f"grouped_{g}_{u}")
+                grouped[g, u] = keep.tile([P, QUARTER, PACK], BF16, align_bytes=64, name=f"grouped_{g}_{u}")
 
-        def interleave(g, j0, j1):
-            for u in range(4):
-                t0 = u * QUARTER
-                src = raw[g, j0][:, :, t0 : t0 + QUARTER]
-                dst = grouped[g, t0][:, :, j0:j1]
-                if j1 - j0 == PACK:
-                    src = src.rearrange("p j (c i) -> p c j i", i=LINE)
-                    dst = dst.rearrange("p (c i) j -> p c j i", i=LINE)
-                else:
-                    src = src.rearrange("p j t -> p t j")
-                if u % 2 == 0:
-                    nc.vector.tensor_copy(out=dst, in_=src)
-                else:
-                    nc.scalar.copy(out=dst, in_=src)
+        def interleave(g, j0, j1, u):
+            src = raw[g, j0, u]
+            dst = grouped[g, u][:, :, j0:j1]
+            if j1 - j0 == PACK:
+                src = src.rearrange("p j (c i) -> p c j i", i=LINE)
+                dst = dst.rearrange("p (c i) j -> p c j i", i=LINE)
+            else:
+                src = src.rearrange("p j t -> p t j")
+            if u % 2 == 0:
+                nc.vector.tensor_copy(out=dst, in_=src)
+            else:
+                nc.scalar.copy(out=dst, in_=src)
 
-        def quantise(g, t0, t1):
-            h = t0 // N_TILE
-            cols = slice(t0 - h * N_TILE, t1 - h * N_TILE)
+        def quantise(g, u):
+            h = u // 2
+            cols = slice((u % 2) * QUARTER, (u % 2 + 1) * QUARTER)
             nc.vector.quantize_mx(
                 out=codes[g, h][:, cols].bitcast(E5M2X4),
                 scales=scale[g, h][:, cols],
-                in_=grouped[g, t0][:].rearrange("p t j -> p (t j)"),
+                in_=grouped[g, u][:].rearrange("p t j -> p (t j)"),
             )
 
         def multiply(g, m, h):
@@ -141,18 +147,27 @@ def tile_mix_dyq_fm_res_kernel(tc, dy, w8_words, w8_scales, w4_words, w4_scales,
                 stop=(g == LAST),
             )
 
-        for g in (2, 0):
-            interleave(g, 0, PACK)
-            for u in range(4):
-                quantise(g, u * QUARTER, (u + 1) * QUARTER)
+        for u in range(4):
+            interleave(2, 0, PACK, u)
+        for u in (1, 2, 3):
+            quantise(2, u)
+        for u in (0, 1):
+            interleave(0, 0, PACK, u)
+        quantise(2, 0)
+        for u in (2, 3):
+            interleave(0, 0, PACK, u)
+        for u in range(4):
+            quantise(0, u)
         for h in range(HALVES):
             for m in range(D_TILES):
                 multiply(2, m, h)
 
-        interleave(LAST, 0, PAIR)
-        interleave(LAST, PAIR, PACK)
         for u in range(4):
-            quantise(LAST, u * QUARTER, (u + 1) * QUARTER)
+            interleave(LAST, 0, PAIR, u)
+        for u in range(4):
+            interleave(LAST, PAIR, PACK, u)
+        for u in range(4):
+            quantise(LAST, u)
 
         for g in (0, LAST):
             for h in range(HALVES):
@@ -177,12 +192,8 @@ def tile_mix_dyq_fm_res_kernel(tc, dy, w8_words, w8_scales, w4_words, w4_scales,
                 in1=res[m][:, first:N_TILE],
                 op=mybir.AluOpType.add,
             )
-            if m == 0:
-                nc.sync.dma_start(out=out[:P, :N_TILE], in_=total[:, :N_TILE])
+            nc.sync.dma_start(out=out[m * P : (m + 1) * P, :N_TILE], in_=total[:, :N_TILE])
             nc.vector.tensor_tensor(
                 out=total[:, N_TILE:], in0=acc[m, 1][:], in1=res[m][:, N_TILE:], op=mybir.AluOpType.add
             )
-            if m == 0:
-                nc.sync.dma_start(out=out[:P, N_TILE:], in_=total[:, N_TILE:])
-            else:
-                nc.sync.dma_start(out=out[m * P : (m + 1) * P, :], in_=total[:])
+            nc.sync.dma_start(out=out[m * P : (m + 1) * P, N_TILE:], in_=total[:, N_TILE:])

@@ -78,13 +78,15 @@ def tile_mix_dyq_fm_res_kernel(tc, dy, w8_words, w8_scales, w4_words, w4_scales,
                 out=w4_scale[q * QUADRANT + 3 : P : 2 * QUADRANT, :].bitcast(I32),
                 in_=w4_scales[0, 4 * q + 3 : 16 : 8, :].bitcast(I32),
             )
+        load_w8_scale(0, 0)
         load_dy(0, 0, PACK, 0, T)
         nc.sync.dma_start(out=w4[:].bitcast(I32), in_=w4_words[0].bitcast(I32))
-        load_dy(LAST, 0, PAIR, 0, T)
-        for s in range(4):
+        for s in range(1, 4):
             load_w8_scale(0, s)
+        load_w8_scale(1, 0)
+        load_dy(LAST, 0, PAIR, 0, T)
         load_dy(LAST, PAIR, PACK, 0, T)
-        for s in range(4):
+        for s in range(1, 4):
             load_w8_scale(1, s)
         load_w8(0)
         load_w8(1)

@@ -25,7 +25,7 @@ QUARTER = 256
 LINE = 4
 LAST = 1
 PAIR = 2
-POOL_COLS = 160
+POOL_COLS = 320
 
 
 def tile_mix_dyq_fm_res_kernel(tc, dy, w8_words, w8_scales, w4_words, w4_scales, r, out):
@@ -64,30 +64,23 @@ def tile_mix_dyq_fm_res_kernel(tc, dy, w8_words, w8_scales, w4_words, w4_scales,
                 in_=w4_scales[0, s:16:4, :].bitcast(I32),
             )
 
-        def load_w8_scale(a, s):
+        def load_w8_scale(s):
             nc.sync.dma_start(
-                out=w8_scale[s:P:QUADRANT, a, :].bitcast(I32),
-                in_=w8_scales[a, s:16:4, :].bitcast(I32),
+                out=w8_scale[s:P:QUADRANT, :, :].bitcast(I32),
+                in_=w8_scales[:, s:16:4, :].rearrange("a q d -> q a d").bitcast(I32),
             )
 
         load_dy(2, 0, PACK, 0, T)
-        for s in range(3):
+        for s in range(4):
             load_w4_scale(s)
-        for q in range(2):
-            nc.sync.dma_start(
-                out=w4_scale[q * QUADRANT + 3 : P : 2 * QUADRANT, :].bitcast(I32),
-                in_=w4_scales[0, 4 * q + 3 : 16 : 8, :].bitcast(I32),
-            )
-        load_w8_scale(0, 0)
+        for s in (0, 1):
+            load_w8_scale(s)
         load_dy(0, 0, PACK, 0, T)
         nc.sync.dma_start(out=w4[:].bitcast(I32), in_=w4_words[0].bitcast(I32))
-        for s in range(1, 4):
-            load_w8_scale(0, s)
-        load_w8_scale(1, 0)
+        for s in (2, 3):
+            load_w8_scale(s)
         load_dy(LAST, 0, PAIR, 0, T)
         load_dy(LAST, PAIR, PACK, 0, T)
-        for s in range(1, 4):
-            load_w8_scale(1, s)
         load_w8(0)
         load_w8(1)
         for m in range(D_TILES):
@@ -194,8 +187,10 @@ def tile_mix_dyq_fm_res_kernel(tc, dy, w8_words, w8_scales, w4_words, w4_scales,
                 in1=res[m][:, first:N_TILE],
                 op=mybir.AluOpType.add,
             )
-            nc.sync.dma_start(out=out[m * P : (m + 1) * P, :N_TILE], in_=total[:, :N_TILE])
+            if m == 0:
+                nc.sync.dma_start(out=out[:P, :N_TILE], in_=total[:, :N_TILE])
             nc.vector.tensor_tensor(
                 out=total[:, N_TILE:], in0=acc[m, 1][:], in1=res[m][:, N_TILE:], op=mybir.AluOpType.add
             )
-            nc.sync.dma_start(out=out[m * P : (m + 1) * P, N_TILE:], in_=total[:, N_TILE:])
+            left = N_TILE if m == 0 else 0
+            nc.sync.dma_start(out=out[m * P : (m + 1) * P, left:], in_=total[:, left:])

@@ -26,6 +26,7 @@ LINE = 4
 LAST = 1
 PAIR = 2
 POOL_COLS = 320
+POOL_COLS_FIRST = 64
 
 
 def tile_mix_dyq_fm_res_kernel(tc, dy, w8_words, w8_scales, w4_words, w4_scales, r, out):
@@ -174,13 +175,12 @@ def tile_mix_dyq_fm_res_kernel(tc, dy, w8_words, w8_scales, w4_words, w4_scales,
                     multiply(g, m, h)
         for m in range(D_TILES):
             total = keep.tile([P, T], F32, align_bytes=256, name=f"total_{m}")
-            first = POOL_COLS if m > 0 else 0
-            if first:
-                drained = keep.tile([P, first], F32, name=f"drained_{m}")
-                nc.scalar.copy(out=drained[:], in_=acc[m, 0][:, :first])
-                nc.gpsimd.tensor_tensor(
-                    out=total[:, :first], in0=drained[:], in1=res[m][:, :first], op=mybir.AluOpType.add
-                )
+            first = POOL_COLS if m > 0 else POOL_COLS_FIRST
+            drained = keep.tile([P, first], F32, name=f"drained_{m}")
+            nc.scalar.copy(out=drained[:], in_=acc[m, 0][:, :first])
+            nc.gpsimd.tensor_tensor(
+                out=total[:, :first], in0=drained[:], in1=res[m][:, :first], op=mybir.AluOpType.add
+            )
             nc.vector.tensor_tensor(
                 out=total[:, first:N_TILE],
                 in0=acc[m, 0][:, first:],

@@ -74,14 +74,13 @@ def tile_mix_dyq_fm_res_kernel(tc, dy, w8_words, w8_scales, w4_words, w4_scales,
         load_dy(2, 0, PACK, 0, T)
         for s in range(4):
             load_w4_scale(s)
-        for s in (0, 1):
-            load_w8_scale(s)
+        load_w8_scale(0)
         load_dy(0, 0, PACK, 0, T)
         nc.sync.dma_start(out=w4[:].bitcast(I32), in_=w4_words[0].bitcast(I32))
-        for s in (2, 3):
-            load_w8_scale(s)
         load_dy(LAST, 0, PAIR, 0, T)
         load_dy(LAST, PAIR, PACK, 0, T)
+        for s in (1, 2, 3):
+            load_w8_scale(s)
         load_w8(0)
         load_w8(1)
         for m in range(D_TILES):

from contextlib import ExitStack

import concourse.mybir as mybir

O, K, M, T = 1024, 1536, 512, 1024
FLOPS = 2 * K * M * T

F32 = mybir.dt.float32
BF16 = mybir.dt.bfloat16
I32 = mybir.dt.int32
U32 = mybir.dt.uint32
U8 = mybir.dt.uint8
E4M3X4 = mybir.dt.float8_e4m3fn_x4
E5M2X4 = mybir.dt.float8_e5m2_x4
E2M1X4 = mybir.dt.float4_e2m1fn_x4

P = 128
PACK = 4
K_PASS = P * PACK
N_TILE = 512
HALVES = T // N_TILE
D_TILES = M // P
QUADRANT = 32
QUARTER = 256
LINE = 4
LAST = 1
PAIR = 2
POOL_COLS = 320
POOL_COLS_FIRST = 64


def tile_mix_dyq_fm_res_kernel(tc, dy, w8_words, w8_scales, w4_words, w4_scales, r, out):
    nc = tc.nc
    with ExitStack() as ctx:
        keep = ctx.enter_context(tc.tile_pool(name="keep", bufs=1))
        psum = ctx.enter_context(tc.psum_pool(name="psum", bufs=1))
        ctx.enter_context(tc.manual_schedule())

        w8_scale = keep.tile([P, 2, M], U8, align_bytes=256)
        w4_scale = keep.tile([P, M], U8, align_bytes=256)
        nc.vector.memset(w4_scale[:].bitcast(I32), 0)
        nc.vector.memset(w8_scale[:].rearrange("p a d -> p (a d)").bitcast(I32), 0)

        w8 = [keep.tile([P, M], U32, align_bytes=256, name=f"w8_{a}") for a in range(2)]
        w4 = keep.tile([P, 2 * M], U8, align_bytes=256)
        res = [keep.tile([P, T], F32, align_bytes=256, name=f"r_{m}") for m in range(D_TILES)]
        raw = {}

        def load_dy(g, j0, j1, t0, t1):
            rows = dy[g * K_PASS : (g + 1) * K_PASS, :].rearrange("(p j) t -> p j t", j=PACK)
            piece = keep.tile([P, j1 - j0, t1 - t0], F32, align_bytes=256, name=f"raw_{g}_{j0}_{t0}")
            for u in range(t0 // QUARTER, t1 // QUARTER):
                raw[g, j0, u] = piece[:, :, u * QUARTER - t0 : (u + 1) * QUARTER - t0]
            nc.sync.dma_start(out=piece[:], in_=rows[:, j0:j1, t0:t1])

        def load_w8(a):
            nc.sync.dma_start(
                out=w8[a][:].bitcast(I32),
                in_=w8_words[a].rearrange("p d i -> p (d i)").bitcast(I32),
            )

        def load_w4_scale(s):
            nc.sync.dma_start(
                out=w4_scale[s:P:QUADRANT, :].bitcast(I32),
                in_=w4_scales[0, s:16:4, :].bitcast(I32),
            )

        def load_w8_scale(s):
            nc.sync.dma_start(
                out=w8_scale[s:P:QUADRANT, :, :].bitcast(I32),
                in_=w8_scales[:, s:16:4, :].rearrange("a q d -> q a d").bitcast(I32),
            )

        load_dy(2, 0, PACK, 0, T)
        for s in range(4):
            load_w4_scale(s)
        load_w8_scale(0)
        load_dy(0, 0, PACK, 0, T)
        nc.sync.dma_start(out=w4[:].bitcast(I32), in_=w4_words[0].bitcast(I32))
        load_dy(LAST, 0, PAIR, 0, T)
        load_dy(LAST, PAIR, PACK, 0, T)
        for s in (1, 2, 3):
            load_w8_scale(s)
        load_w8(0)
        load_w8(1)
        for m in range(D_TILES):
            nc.sync.dma_start(out=res[m][:], in_=r[m * P : (m + 1) * P, :])

        acc = {}
        for m in range(D_TILES):
            for h in range(HALVES):
                acc[m, h] = psum.tile([P, N_TILE], F32, name=f"acc_{m}_{h}")

        codes = {}
        scale = {}
        for g in range(3):
            for h in range(HALVES):
                codes[g, h] = keep.tile([P, N_TILE], U32, align_bytes=64, name=f"codes_{g}_{h}")
                scale[g, h] = keep.tile([P, N_TILE], U8, align_bytes=64, name=f"scale_{g}_{h}")
        grouped = {}
        for g in range(3):
            for u in range(4):
                grouped[g, u] = keep.tile([P, QUARTER, PACK], BF16, align_bytes=64, name=f"grouped_{g}_{u}")

        def interleave(g, j0, j1, u):
            src = raw[g, j0, u]
            dst = grouped[g, u][:, :, j0:j1]
            if j1 - j0 == PACK:
                src = src.rearrange("p j (c i) -> p c j i", i=LINE)
                dst = dst.rearrange("p (c i) j -> p c j i", i=LINE)
            else:
                src = src.rearrange("p j t -> p t j")
            if u % 2 == 0:
                nc.vector.tensor_copy(out=dst, in_=src)
            else:
                nc.scalar.copy(out=dst, in_=src)

        def quantise(g, u):
            h = u // 2
            cols = slice((u % 2) * QUARTER, (u % 2 + 1) * QUARTER)
            nc.vector.quantize_mx(
                out=codes[g, h][:, cols].bitcast(E5M2X4),
                scales=scale[g, h][:, cols],
                in_=grouped[g, u][:].rearrange("p t j -> p (t j)"),
            )

        def multiply(g, m, h):
            d_cols = slice(m * P, (m + 1) * P)
            if g < 2:
                lhsT = w8[g][:, d_cols].bitcast(E4M3X4)
                lhsT_scale = w8_scale[:, g, d_cols]
            else:
                lhsT = w4[:, 2 * m * P : 2 * (m + 1) * P].bitcast(E2M1X4)
                lhsT_scale = w4_scale[:, d_cols]
            nc.tensor.matmul_mx(
                out=acc[m, h][:],
                lhsT=lhsT,
                lhsT_scale=lhsT_scale,
                rhs=codes[g, h][:].bitcast(E5M2X4),
                rhs_scale=scale[g, h][:],
                start=(g == 2),
                stop=(g == LAST),
            )

        for u in range(4):
            interleave(2, 0, PACK, u)
        for u in (1, 2, 3):
            quantise(2, u)
        for u in (0, 1):
            interleave(0, 0, PACK, u)
        quantise(2, 0)
        for u in (2, 3):
            interleave(0, 0, PACK, u)
        for u in range(4):
            quantise(0, u)
        for h in range(HALVES):
            for m in range(D_TILES):
                multiply(2, m, h)

        for u in range(4):
            interleave(LAST, 0, PAIR, u)
        for u in range(4):
            interleave(LAST, PAIR, PACK, u)
        for u in range(4):
            quantise(LAST, u)

        for g in (0, LAST):
            for h in range(HALVES):
                for m in (0, 1):
                    multiply(g, m, h)
        for m in (2, 3):
            for h in range(HALVES):
                for g in (0, LAST):
                    multiply(g, m, h)
        for m in range(D_TILES):
            total = keep.tile([P, T], F32, align_bytes=256, name=f"total_{m}")
            first = POOL_COLS if m > 0 else POOL_COLS_FIRST
            drained = keep.tile([P, first], F32, name=f"drained_{m}")
            nc.scalar.copy(out=drained[:], in_=acc[m, 0][:, :first])
            nc.gpsimd.tensor_tensor(
                out=total[:, :first], in0=drained[:], in1=res[m][:, :first], op=mybir.AluOpType.add
            )
            nc.vector.tensor_tensor(
                out=total[:, first:N_TILE],
                in0=acc[m, 0][:, first:],
                in1=res[m][:, first:N_TILE],
                op=mybir.AluOpType.add,
            )
            if m == 0:
                nc.sync.dma_start(out=out[:P, :N_TILE], in_=total[:, :N_TILE])
            nc.vector.tensor_tensor(
                out=total[:, N_TILE:], in0=acc[m, 1][:], in1=res[m][:, N_TILE:], op=mybir.AluOpType.add
            )
            left = N_TILE if m == 0 else 0
            nc.sync.dma_start(out=out[m * P : (m + 1) * P, left:], in_=total[:, left:])
